import numpy as np
import ml_dtypes


def mxq(x, axis, fmt="e4m3"):
    dtype, down = {"e4m3": (ml_dtypes.float8_e4m3fn, 7), "e5m2": (ml_dtypes.float8_e5m2, 14)}[fmt]
    v = np.moveaxis(np.asarray(x, np.float32).astype(ml_dtypes.bfloat16).astype(np.float64), axis, -1)
    blocks = v.reshape(v.shape[:-1] + (-1, 32))
    amax = np.abs(blocks).max(-1, keepdims=True)
    byte = np.maximum(np.where(amax > 0, np.frexp(amax)[1] - 1 + 127, 0) - down, 1)
    scale = np.exp2(byte - 127.0)
    codes = (blocks / scale).astype(np.float32).astype(dtype).astype(np.float64)
    return np.moveaxis((codes * scale).reshape(v.shape), -1, axis)


WIDE = False


def mx_kscale(k):
    if not WIDE:
        return np.ones(k)
    levels = np.array([10, -10, 5, -5, 0])
    if k % 512:
        return np.exp2(np.random.permutation(np.resize(levels, k // 32))).repeat(32)
    a = np.empty((k // 512, 16))
    for p in range(k // 512):
        a[p, :8] = np.random.permutation(np.resize(levels, 8))
        for g in range(8):
            far = levels[np.abs(levels - a[p, g]) >= 10]
            a[p, g + 8] = far[np.random.randint(len(far))]
    return np.exp2(a.ravel()).repeat(32)


BF16 = ml_dtypes.bfloat16


def bf(x):
    return np.asarray(x, np.float32).astype(BF16)


def f64(x):
    return np.asarray(x).astype(np.float64)


E2M1 = np.array([0.0, 0.5, 1.0, 1.5, 2.0, 3.0, 4.0, 6.0, -0.0, -0.5, -1.0, -1.5, -2.0, -3.0, -4.0, -6.0])


def pack_weight(w, fmt):
    k, n = w.shape
    w = f64(bf(w)).reshape(k // 32, 32, n)
    amax = np.abs(w).max(1)
    if fmt == "e4m3":
        byte = np.frexp(amax)[1] - 1 + 127 - 7
    else:
        mant, ex = np.frexp(amax / 6.0)
        byte = np.where(mant > 0.5, ex, ex - 1) + 127
    byte = np.clip(np.where(amax > 0, byte, 1), 1, 254)
    scaled = (w * np.exp2(127.0 - byte)[:, None, :]).reshape(k, n).astype(np.float32)
    by_word = np.ascontiguousarray(scaled.reshape(k // 512, 128, 4, n).transpose(0, 1, 3, 2))
    if fmt == "e4m3":
        words = by_word.astype(ml_dtypes.float8_e4m3fn).view(np.uint8)
    else:
        c = by_word.astype(ml_dtypes.float4_e2m1fn).view(np.uint8) & 0xF
        words = c[..., 0::2] | (c[..., 1::2] << 4)
    return np.ascontiguousarray(words), np.ascontiguousarray(byte.astype(np.uint8).reshape(k // 512, 16, n))


def unpack_weight(words, scales, fmt):
    g, p, n, _ = words.shape
    if fmt == "e4m3":
        vals = np.ascontiguousarray(words).view(ml_dtypes.float8_e4m3fn).astype(np.float64)
    else:
        nib = np.empty((g, p, n, 4), np.uint8)
        nib[..., 0::2] = words & 0xF
        nib[..., 1::2] = words >> 4
        vals = E2M1[nib]
    vals = vals * np.repeat(np.exp2(scales.astype(np.float64) - 127.0), 8, axis=1)[..., None]
    return vals.transpose(0, 1, 3, 2).reshape(g * 512, n)
def pack4(w):
    words, scales = pack_weight(w, "e2m1")
    return words.reshape(words.shape[0], 128, -1), scales


def unpack4(words, scales):
    return unpack_weight(words.reshape(words.shape[0], 128, -1, 2), scales, "e2m1")


E4M3FN = np.array([(-1.0 if i & 128 else 1.0) * ((1.0 + (i & 7) / 8.0) * 2.0 ** (((i >> 3) & 15) - 7) if i & 120 else (i & 7) * 2.0 ** -9) for i in range(256)])


def e4m3fn_bytes(y):
    return np.clip(np.asarray(y, np.float64), -448.0, 448.0).astype(np.float32).astype(ml_dtypes.float8_e4m3fn).view(np.uint8)


def e4m3fn_values(b):
    return E4M3FN[b]


B, HH, WW, D, F, KH, KW = 1, 32, 32, 512, 1024, 3, 3
F2 = 2 * F


def silu(z):
    return z / (1.0 + np.exp(-z))


def depthwise_corr(u, wd):
    rows, cols = u.shape[1], u.shape[2]
    ph, pw = KH // 2, KW // 2
    upad = np.pad(u, ((0, 0), (ph, ph), (pw, pw), (0, 0)))
    c = np.zeros_like(u)
    for r in range(KH):
        band = upad[:, r:r + rows, :, :]
        for t in range(KW):
            c = c + wd[r, t] * band[:, :, t:t + cols, :]
    return c


def draw0():
    s, t = mx_kscale(D), mx_kscale(F)
    x = bf(np.random.standard_normal((B, HH, WW, D)) * s)
    w1_words, w1_scales = pack4(np.random.standard_normal((D, F2)) / np.sqrt(D) / s[:, None])
    b1 = bf(np.random.standard_normal(F2) * 0.3)
    wd = bf(np.random.standard_normal((KH, KW, F2)) * 0.5)
    gain = bf((1.0 + 0.1 * np.random.standard_normal(F)) * t)
    w2_words, w2_scales = pack4(np.random.standard_normal((F, D)) * 2.0 / np.sqrt(F) / t[:, None])
    return {"x": x,
            "w1_words": w1_words,
            "w1_scales": w1_scales,
            "b1": b1,
            "wd": wd,
            "gain": gain,
            "w2_words": w2_words,
            "w2_scales": w2_scales}


def core(x, w1_words, w1_scales, b1, wd, gain, w2_words, w2_scales):
    f = gain.shape[0]
    h = (mxq(f64(x), 3, "e4m3") @ unpack4(w1_words, w1_scales)) + f64(b1)
    u = silu(h)
    c = depthwise_corr(u, f64(wd))
    ca = c[..., :f]
    cb = c[..., f:]
    g = f64(gain) * ca * silu(cb)
    return mxq(g, 3, "e4m3") @ unpack4(w2_words, w2_scales)


def setup_inputs():
    drawn = draw0()
    full = np.asarray(drawn['x']).astype(np.float64)
    scale = (np.abs(full).reshape(1, 32, 32, 4, 128).max(axis=(4,)) / 448.0).astype(np.float32)
    given = {}
    for key, value in drawn.items():
        if key == 'x':
            given['x_bytes'] = e4m3fn_bytes(full / np.repeat(scale.astype(np.float64), 128, axis=3))
            given['x_scale'] = scale
        else:
            given[key] = value
    return given


def reference(x_bytes, x_scale, w1_words, w1_scales, b1, wd, gain, w2_words, w2_scales):
    return core(e4m3fn_values(x_bytes) * np.repeat(x_scale.astype(np.float64), 128, axis=3), w1_words, w1_scales, b1, wd, gain, w2_words, w2_scales)

@@ -1,0 +1,366 @@
+from contextlib import ExitStack
+
+import concourse.mybir as mybir
+from concourse.masks import make_identity
+
+F32 = mybir.dt.float32
+BF16 = mybir.dt.bfloat16
+U8 = mybir.dt.uint8
+U32 = mybir.dt.uint32
+I32 = mybir.dt.int32
+FP8 = mybir.dt.float8_e4m3fn
+FP8X4 = mybir.dt.float8_e4m3fn_x4
+FP4X4 = mybir.dt.float4_e2m1fn_x4
+ACT = mybir.ActivationFunctionType
+MULT = mybir.AluOpType.mult
+ADD = mybir.AluOpType.add
+
+P = 128
+T = 1024
+D = 512
+F = 1024
+FLOPS = 2 * T * D * 2 * F + 2 * T * F * D + 2 * 9 * T * 2 * F
+
+UNITS_A = ([0, 1, 2], [[3, 7], [4, 8], [5], [6]])
+UNITS_B = ([0, 1, 2], [[3, 6], [4, 7], [5, 8]])
+
+
+def tile_sanamixffndepthwiseglu_d1p_kernel(tc, x_bytes, x_scale, w1_words, w1_scales, b1, wd, gain, w2_words, w2_scales, out):
+    nc = tc.nc
+    with ExitStack() as ctx:
+        const = ctx.enter_context(tc.tile_pool(name="const", bufs=1))
+        work = ctx.enter_context(tc.tile_pool(name="work", bufs=3))
+        psum = ctx.enter_context(tc.psum_pool(name="psum", bufs=1))
+        ctx.enter_context(tc.manual_schedule())
+
+        xb = const.tile([P, 8, D], U8, name="xb", align_bytes=64)
+        xs = const.tile([P, 8, 4], F32, name="xs")
+        w1 = const.tile([P, 4096], U8, name="w1", align_bytes=64)
+        w1s = const.tile([P, 2 * F], U8, name="w1s", align_bytes=64)
+        w2 = const.tile([P, 2, 1024], U8, name="w2", align_bytes=64)
+        w2s = const.tile([P, 2, D], U8, name="w2s", align_bytes=64)
+        prm_a = const.tile([P, P], BF16, name="prm_a")
+        prm_b = const.tile([P, P], BF16, name="prm_b")
+        par = const.tile([P, 168], F32, name="par")
+        wg = const.tile([P, 9, 8], F32, name="wg")
+        warm = const.tile([P, 1], F32, name="warm")
+        identf = const.tile([P, P], F32, name="identf", align_bytes=64)
+        identb = const.tile([P, P], BF16, name="identb", align_bytes=64)
+        perm = const.tile([P, P], F32, name="perm", align_bytes=64)
+        xw = const.tile([P, 8, D], BF16, name="xw", align_bytes=64)
+        xq = const.tile([P, T], U32, name="xq", align_bytes=64)
+        xqs = const.tile([P, T], U8, name="xqs", align_bytes=64)
+        u0 = const.tile([P, 34, 34], F32, name="u0", align_bytes=64)
+        u1 = const.tile([P, 34, 34], F32, name="u1", align_bytes=64)
+        u2 = const.tile([P, 34, 34], F32, name="u2", align_bytes=64)
+        us = [u0, u1, u2]
+        g = const.tile([P, 8, 2, 2, 256], BF16, name="g", align_bytes=64)
+        gq = const.tile([P, 2, T], U32, name="gq", align_bytes=64)
+        gqs = const.tile([P, 2, T], U8, name="gqs", align_bytes=64)
+
+        xv = x_bytes.rearrange("o a b k -> (o a b) k").rearrange("(i p) k -> p i k", p=P)
+        xsv = x_scale.rearrange("o a b j -> (o a b) j").rearrange("(i p) j -> p i j", p=P)
+        ov = out.rearrange("o a b n -> (o a b) n")
+        wdv = wd.rearrange("r t (c p) -> (r t c) p", p=P)
+
+        nc.scalar.dma_start(out=xs[:], in_=xsv)
+        for m in range(4):
+            nc.sync.dma_start(out=xb[:, 2 * m : 2 * m + 2, :], in_=xv[:, 2 * m : 2 * m + 2, :])
+        nc.vector.memset(warm[:], 0.0)
+        nc.vector.memset(prm_b[:], 0.0)
+        nc.vector.memset(w1s[:].bitcast(I32), 0)
+        nc.vector.memset(w2s[:].rearrange("p g n -> p (g n)").bitcast(I32), 0)
+        nc.scalar.dma_start(out=prm_a[:], in_=wdv[0:P, :])
+        nc.scalar.dma_start(out=prm_b[0:16, :], in_=wdv[P : P + 16, :])
+        nc.scalar.dma_start(out=prm_b[16:32, :], in_=b1.rearrange("(c p) -> c p", p=P))
+        nc.scalar.dma_start(out=prm_b[32:40, :], in_=gain.rearrange("(c p) -> c p", p=P))
+        nc.scalar.activation(out=warm[:], in_=warm[:], func=ACT.Silu)
+        nc.sync.dma_start(out=w1[:].bitcast(I32), in_=w1_words[0].bitcast(I32))
+        for q in range(4):
+            nc.sync.dma_start(out=w1s[32 * q : 32 * q + 4, :].bitcast(I32), in_=w1_scales[0, 4 * q : 4 * q + 4, :].bitcast(I32))
+        nc.sync.dma_start(out=w2[:].rearrange("p g n -> p (g n)").bitcast(I32).rearrange("p (g n) -> p g n", g=2), in_=w2_words.bitcast(I32).rearrange("g p n -> p g n"))
+        for q in range(4):
+            nc.sync.dma_start(
+                out=w2s[32 * q : 32 * q + 4, :, :].rearrange("p g n -> p (g n)").bitcast(I32).rearrange("p (g n) -> p g n", g=2),
+                in_=w2_scales.bitcast(I32)[:, 4 * q : 4 * q + 4, :].rearrange("g q n -> q g n"),
+            )
+
+        make_identity(nc, identf[:])
+        nc.gpsimd.memset(u0[:], 0.0)
+        make_identity(nc, identb[:])
+        nc.gpsimd.memset(u1[:], 0.0)
+        nc.gpsimd.memset(u2[:], 0.0)
+
+        def widen(m):
+            for i in (2 * m, 2 * m + 1):
+                for j in range(4):
+                    cols = slice(P * j, P * j + P)
+                    if j < 3:
+                        nc.vector.tensor_scalar(out=xw[:, i, cols], in0=xb[:, i, cols].bitcast(FP8), scalar1=xs[:, i, j : j + 1], scalar2=None, op0=MULT)
+                    else:
+                        nc.scalar.activation(out=xw[:, i, cols], in_=xb[:, i, cols].bitcast(FP8), func=ACT.Copy, scale=xs[:, i, j : j + 1])
+
+        xt = {}
+        xg = {}
+
+        def x_turn(m):
+            t = psum.tile([P, 2, 2, P], F32, name="xt_%d" % m, tag="acc", bufs=5)
+            xt[m] = t
+            for i2 in range(2):
+                words = xw[:, 2 * m + i2, :].bitcast(F32)
+                for u in range(2):
+                    nc.tensor.transpose(t[:, i2, u, :], words[:, u:256:2], identf[:])
+
+        def turn_copy(src, name):
+            dst = work.tile([P, 1024], BF16, name=name, tag="grouped", bufs=3, align_bytes=64)
+            nc.scalar.copy(
+                out=dst[:].bitcast(F32).rearrange("p (i r u) -> p i r u", i=2, u=2),
+                in_=src[:].rearrange("p i u r -> p i r u"),
+            )
+            return dst
+
+        def x_copy(m):
+            xg[m] = turn_copy(xt[m], "xg_%d" % m)
+
+        def x_quant(m):
+            cols = slice(256 * m, 256 * m + 256)
+            nc.vector.quantize_mx(out=xq[:, cols].bitcast(FP8X4), scales=xqs[:, cols], in_=xg[m][:])
+
+        order = []
+        for pr in range(8):
+            order += [pr, 8 + pr]
+
+        hs = {}
+
+        def mx1(n, half):
+            c = order[n]
+            h = psum.tile([P, 512], F32, name="h_%d_%d" % (n, half), tag="h%d" % half, bufs=1)
+            hs[n, half] = h
+            cols = slice(512 * half, 512 * half + 512)
+            nc.tensor.matmul_mx(
+                out=h[:],
+                lhsT=w1[:, 256 * c : 256 * c + 256].bitcast(FP4X4),
+                lhsT_scale=w1s[:, P * c : P * c + P],
+                rhs=xq[:, cols].bitcast(FP8X4),
+                rhs_scale=xqs[:, cols],
+                start=True,
+                stop=True,
+            )
+
+        def silu1(n, half):
+            c = order[n]
+            nc.scalar.activation(
+                out=us[n % 3][:, 1 + 16 * half : 17 + 16 * half, 1:33],
+                in_=hs[n, half][:].rearrange("p (r w) -> p r w", w=32),
+                func=ACT.Silu,
+                bias=par[:, 144 + c : 145 + c],
+            )
+
+        units = {}
+
+        def tap_weight(n, tap):
+            c = order[n]
+            if c < 8:
+                return wg[:, tap, c : c + 1]
+            return par[:, 16 * tap + c : 16 * tap + c + 1]
+
+        def window(n, tap):
+            r, t = divmod(tap, 3)
+            return us[n % 3][:, r : r + 32, t : t + 32]
+
+        def new_unit(n, k):
+            t = work.tile([P, T], F32, name="unit_%d_%d" % (n, k), tag="unit%d" % k, bufs=3, align_bytes=64)
+            units[n].append(t)
+            return t
+
+        def rows(t):
+            return t[:].rearrange("p (r w) -> p r w", w=32)
+
+        def spec(n):
+            return UNITS_A if n % 2 == 0 else UNITS_B
+
+        def alloc_units(n):
+            units[n] = []
+            s, v = spec(n)
+            for k in range(len(s) + len(v)):
+                new_unit(n, k)
+
+        def s_product(n, k):
+            tap = spec(n)[0][k]
+            nc.scalar.activation(out=rows(units[n][k]), in_=window(n, tap), func=ACT.Copy, scale=tap_weight(n, tap))
+
+        def v_products(n):
+            s, v = spec(n)
+            depth = max(len(taps) for taps in v)
+            for d in range(depth):
+                for k, taps in enumerate(v):
+                    if d >= len(taps):
+                        continue
+                    unit = rows(units[n][len(s) + k])
+                    if d == 0:
+                        nc.vector.tensor_scalar(out=unit, in0=window(n, taps[0]), scalar1=tap_weight(n, taps[0]), scalar2=None, op0=MULT)
+                    else:
+                        nc.vector.scalar_tensor_tensor(out=unit, in0=window(n, taps[d]), scalar=tap_weight(n, taps[d]), in1=unit, op0=MULT, op1=ADD)
+
+        accs = {}
+
+        def gather(n, half):
+            acc = psum.tile([P, 512], F32, name="acc_%d_%d" % (n, half), tag="acc", bufs=5)
+            accs[n, half] = acc
+            count = len(units[n])
+            for j in range(4):
+                tok = slice(512 * half + P * j, 512 * half + P * j + P)
+                for k in range(count):
+                    nc.tensor.matmul(acc[:, P * j : P * j + P], lhsT=units[n][k][:, tok], rhs=perm[:], start=(k == 0), stop=(k == count - 1), is_transpose=True)
+
+        sgs = {}
+
+        def gate_silu(pr, half):
+            sg = work.tile([P, 512], F32, name="sg_%d_%d" % (pr, half), tag="sg", bufs=3, align_bytes=64)
+            sgs[pr, half] = sg
+            nc.scalar.activation(out=sg[:], in_=accs[2 * pr + 1, half][:], func=ACT.Silu)
+
+        def gate_mul(pr, half):
+            q, c4 = divmod(pr, 4)
+            nc.vector.tensor_tensor(
+                out=g[:, 4 * half : 4 * half + 4, q, :, 64 * c4 : 64 * c4 + 64],
+                in0=accs[2 * pr, half][:].rearrange("p (i u w) -> p i u w", i=4, u=2),
+                in1=sgs[pr, half][:].rearrange("p (i u w) -> p i u w", i=4, u=2),
+                op=MULT,
+            )
+
+        gt = {}
+        gg = {}
+
+        def g_turn(q, m):
+            t = psum.tile([P, 2, 2, P], F32, name="gt_%d_%d" % (q, m), tag="tp", bufs=1)
+            gt[q, m] = t
+            for i2 in range(2):
+                for u in range(2):
+                    nc.tensor.transpose(t[:, i2, u, :], g[:, 2 * m + i2, q, u, :].bitcast(F32), identf[:])
+
+        def g_copy(q, m):
+            gg[q, m] = turn_copy(gt[q, m], "gg_%d_%d" % (q, m))
+
+        def g_quant(q, m):
+            cols = slice(256 * m, 256 * m + 256)
+            nc.vector.quantize_mx(out=gq[:, q, cols].bitcast(FP8X4), scales=gqs[:, q, cols], in_=gg[q, m][:])
+
+        outs = {}
+        out_tags = [("h0", 1), ("h1", 1), ("acc", 5), ("acc", 5)]
+
+        def mx2(i):
+            tag, bufs = out_tags[i % 4]
+            o = psum.tile([P, D], F32, name="o_%d" % i, tag=tag, bufs=bufs)
+            outs[i] = o
+            tok = slice(P * i, P * i + P)
+            for q in range(2):
+                nc.tensor.matmul_mx(
+                    out=o[:],
+                    lhsT=gq[:, q, tok].bitcast(FP8X4),
+                    lhsT_scale=gqs[:, q, tok],
+                    rhs=w2[:, q, :].bitcast(FP4X4),
+                    rhs_scale=w2s[:, q, :],
+                    start=(q == 0),
+                    stop=(q == 1),
+                )
+
+        def store(i):
+            ob = work.tile([P, D], F32, name="ob_%d" % i, tag="ob", bufs=8, align_bytes=64)
+            if i % 2 == 0:
+                nc.scalar.copy(out=ob[:], in_=outs[i][:])
+            else:
+                nc.vector.tensor_copy(out=ob[:], in_=outs[i][:])
+            nc.sync.dma_start(out=ov[P * i : P * i + P, :], in_=ob[:])
+
+        widen(0)
+        widen(1)
+        x_turn(0)
+        x_turn(1)
+        x_copy(0)
+        widen(2)
+        x_quant(0)
+        x_turn(2)
+        x_copy(1)
+        widen(3)
+        x_quant(1)
+        x_turn(3)
+        x_copy(2)
+        pt = psum.tile([P, 2, P], BF16, name="pt", tag="tp", bufs=1)
+        nc.tensor.transpose(pt[:, 0, :], prm_a[:], identb[:])
+        nc.tensor.transpose(pt[:, 1, :], prm_b[:], identb[:])
+        nc.vector.tensor_copy(out=par[:], in_=pt[:].rearrange("p a b -> p (a b)")[:, 0:168])
+        mx1(0, 0)
+        x_copy(3)
+        x_quant(2)
+        nc.vector.tensor_tensor(
+            out=wg[:],
+            in0=par[:, 0:144].rearrange("p (k c) -> p k c", c=16)[:, :, 0:8],
+            in1=par[:, 160:168].unsqueeze(1).to_broadcast([P, 9, 8]),
+            op=MULT,
+        )
+        silu1(0, 0)
+        x_quant(3)
+        nc.vector.tensor_copy(out=perm[:].rearrange("q (u p e) -> q u p e", u=2, e=2), in_=identf[:].rearrange("q (p u e) -> q u p e", u=2, e=2))
+        mx1(0, 1)
+        silu1(0, 1)
+        mx1(1, 0)
+        mx1(1, 1)
+
+        for n in range(17):
+            late = n - 2
+            if late >= 1 and late % 2 == 1:
+                gate_silu(late // 2, 1)
+                gate_mul(late // 2, 1)
+            if 10 <= n <= 13:
+                g_copy(0, n - 10)
+                g_quant(0, n - 10)
+            if n < 16:
+                alloc_units(n)
+                s_product(n, 0)
+            if n < 15:
+                silu1(n + 1, 0)
+                silu1(n + 1, 1)
+            if n >= 1:
+                gather(n - 1, 0)
+            if n < 14:
+                mx1(n + 2, 0)
+                mx1(n + 2, 1)
+            if n < 16:
+                s_product(n, 1)
+                v_products(n)
+            if n >= 1 and (n - 1) % 2 == 1:
+                gate_silu((n - 1) // 2, 0)
+                gate_mul((n - 1) // 2, 0)
+            if n >= 1:
+                gather(n - 1, 1)
+            if n < 16:
+                s_product(n, 2)
+            if 9 <= n <= 12:
+                g_turn(0, n - 9)
+
+        g_turn(1, 0)
+        g_copy(1, 0)
+        g_quant(1, 0)
+        gate_silu(7, 1)
+        gate_mul(7, 1)
+        g_turn(1, 1)
+        g_copy(1, 1)
+        g_quant(1, 1)
+        mx2(0)
+        mx2(1)
+        g_turn(1, 2)
+        g_copy(1, 2)
+        g_quant(1, 2)
+        store(0)
+        store(1)
+        mx2(2)
+        mx2(3)
+        g_turn(1, 3)
+        g_copy(1, 3)
+        g_quant(1, 3)
+        for i in range(4, 8):
+            mx2(i)
+            store(i - 2)
+        store(6)
+        store(7)

@@ -21,8 +21,16 @@ D = 512
 F = 1024
 FLOPS = 2 * T * D * 2 * F + 2 * T * F * D + 2 * 9 * T * 2 * F
 
-UNITS_A = ([0, 1, 2], [[3, 7], [4, 8], [5], [6]])
-UNITS_B = ([0, 1, 2], [[3, 6], [4, 7], [5, 8]])
+PLAN = [(3, 2), (4, 2)] * 8
+DUMMY = True
+VCOPY = True
+
+
+def split_taps(s, v):
+    lists = [[s + k] for k in range(v)]
+    for k, tap in enumerate(range(s + v, 9)):
+        lists[k % v].append(tap)
+    return list(range(s)), lists
 
 
 def tile_sanamixffndepthwiseglu_d1p_kernel(tc, x_bytes, x_scale, w1_words, w1_scales, b1, wd, gain, w2_words, w2_scales, out):
@@ -111,12 +119,14 @@ def tile_sanamixffndepthwiseglu_d1p_kernel(tc, x_bytes, x_scale, w1_words, w1_sc
                 for u in range(2):
                     nc.tensor.transpose(t[:, i2, u, :], words[:, u:256:2], identf[:])
 
-        def turn_copy(src, name):
+        def turn_copy(src, name, vector=False):
             dst = work.tile([P, 1024], BF16, name=name, tag="grouped", bufs=3, align_bytes=64)
-            nc.scalar.copy(
-                out=dst[:].bitcast(F32).rearrange("p (i r u) -> p i r u", i=2, u=2),
-                in_=src[:].rearrange("p i u r -> p i r u"),
-            )
+            o = dst[:].bitcast(F32).rearrange("p (i r u) -> p i r u", i=2, u=2)
+            s = src[:].rearrange("p i u r -> p i r u")
+            if vector:
+                nc.vector.tensor_copy(out=o, in_=s)
+            else:
+                nc.scalar.copy(out=o, in_=s)
             return dst
 
         def x_copy(m):
@@ -132,10 +142,18 @@ def tile_sanamixffndepthwiseglu_d1p_kernel(tc, x_bytes, x_scale, w1_words, w1_sc
 
         hs = {}
 
+        def h_tile(n, half):
+            hs[n, half] = psum.tile([P, 512], F32, name="h_%d_%d" % (n, half), tag="h%d" % half, bufs=1)
+
+        def dummy(n):
+            h_tile(n, 1)
+            nc.tensor.matmul(hs[n, 1][:], lhsT=identb[:], rhs=xw[:, 0, :], start=True, stop=True)
+
         def mx1(n, half):
             c = order[n]
-            h = psum.tile([P, 512], F32, name="h_%d_%d" % (n, half), tag="h%d" % half, bufs=1)
-            hs[n, half] = h
+            if (n, half) not in hs:
+                h_tile(n, half)
+            h = hs[n, half]
             cols = slice(512 * half, 512 * half + 512)
             nc.tensor.matmul_mx(
                 out=h[:],
@@ -164,20 +182,20 @@ def tile_sanamixffndepthwiseglu_d1p_kernel(tc, x_bytes, x_scale, w1_words, w1_sc
                 return wg[:, tap, c : c + 1]
             return par[:, 16 * tap + c : 16 * tap + c + 1]
 
-        def window(n, tap):
+        def window(n, tap, lo, hi):
             r, t = divmod(tap, 3)
-            return us[n % 3][:, r : r + 32, t : t + 32]
+            return us[n % 3][:, r + lo : r + hi, t : t + 32]
 
         def new_unit(n, k):
             t = work.tile([P, T], F32, name="unit_%d_%d" % (n, k), tag="unit%d" % k, bufs=3, align_bytes=64)
             units[n].append(t)
             return t
 
-        def rows(t):
-            return t[:].rearrange("p (r w) -> p r w", w=32)
+        def rows(t, lo, hi):
+            return t[:, 32 * lo : 32 * hi].rearrange("p (r w) -> p r w", w=32)
 
         def spec(n):
-            return UNITS_A if n % 2 == 0 else UNITS_B
+            return split_taps(PLAN[n][0], PLAN[n][1])
 
         def alloc_units(n):
             units[n] = []
@@ -185,47 +203,59 @@ def tile_sanamixffndepthwiseglu_d1p_kernel(tc, x_bytes, x_scale, w1_words, w1_sc
             for k in range(len(s) + len(v)):
                 new_unit(n, k)
 
-        def s_product(n, k):
-            tap = spec(n)[0][k]
-            nc.scalar.activation(out=rows(units[n][k]), in_=window(n, tap), func=ACT.Copy, scale=tap_weight(n, tap))
+        def s_product(n, k, lo=0, hi=32):
+            if k < len(spec(n)[0]):
+                tap = spec(n)[0][k]
+                nc.scalar.activation(out=rows(units[n][k], lo, hi), in_=window(n, tap, lo, hi), func=ACT.Copy, scale=tap_weight(n, tap))
 
-        def v_products(n):
+        def v_products(n, lo, hi, extra=()):
             s, v = spec(n)
-            depth = max(len(taps) for taps in v)
-            for d in range(depth):
+            work_list = []
+            for d in range(max(len(taps) for taps in v)):
                 for k, taps in enumerate(v):
-                    if d >= len(taps):
-                        continue
-                    unit = rows(units[n][len(s) + k])
-                    if d == 0:
-                        nc.vector.tensor_scalar(out=unit, in0=window(n, taps[0]), scalar1=tap_weight(n, taps[0]), scalar2=None, op0=MULT)
-                    else:
-                        nc.vector.scalar_tensor_tensor(out=unit, in0=window(n, taps[d]), scalar=tap_weight(n, taps[d]), in1=unit, op0=MULT, op1=ADD)
+                    if d < len(taps):
+                        work_list.append((k, d, taps[d]))
+            for pos, (k, d, tap) in enumerate(work_list):
+                unit = rows(units[n][len(s) + k], lo, hi)
+                if d == 0:
+                    nc.vector.tensor_scalar(out=unit, in0=window(n, tap, lo, hi), scalar1=tap_weight(n, tap), scalar2=None, op0=MULT)
+                else:
+                    nc.vector.scalar_tensor_tensor(out=unit, in0=window(n, tap, lo, hi), scalar=tap_weight(n, tap), in1=unit, op0=MULT, op1=ADD)
+                for at, fn in extra:
+                    if at == pos:
+                        fn()
 
         accs = {}
 
-        def gather(n, half):
-            acc = psum.tile([P, 512], F32, name="acc_%d_%d" % (n, half), tag="acc", bufs=5)
-            accs[n, half] = acc
+        def gather(n, part, parts=2):
+            tiles = 8 // parts
+            acc = psum.tile([P, P * tiles], F32, name="acc_%d_%d" % (n, part), tag="acc", bufs=5)
+            accs[n, part] = acc
             count = len(units[n])
-            for j in range(4):
-                tok = slice(512 * half + P * j, 512 * half + P * j + P)
+            for j in range(tiles):
+                lo = P * (tiles * part + j)
                 for k in range(count):
-                    nc.tensor.matmul(acc[:, P * j : P * j + P], lhsT=units[n][k][:, tok], rhs=perm[:], start=(k == 0), stop=(k == count - 1), is_transpose=True)
+                    nc.tensor.matmul(
+                        acc[:, P * j : P * j + P], lhsT=units[n][k][:, lo : lo + P], rhs=perm[:],
+                        start=(k == 0), stop=(k == count - 1), is_transpose=True,
+                    )
 
         sgs = {}
 
-        def gate_silu(pr, half):
-            sg = work.tile([P, 512], F32, name="sg_%d_%d" % (pr, half), tag="sg", bufs=3, align_bytes=64)
-            sgs[pr, half] = sg
-            nc.scalar.activation(out=sg[:], in_=accs[2 * pr + 1, half][:], func=ACT.Silu)
+        def gate_silu(pr, part, parts=2):
+            width = T // parts
+            sg = work.tile([P, width], F32, name="sg_%d_%d" % (pr, part), tag="sg", bufs=4, align_bytes=64)
+            sgs[pr, part] = sg
+            nc.scalar.activation(out=sg[:], in_=accs[2 * pr + 1, part][:], func=ACT.Silu)
 
-        def gate_mul(pr, half):
+        def gate_mul(pr, part, parts=2):
             q, c4 = divmod(pr, 4)
+            tiles = 8 // parts
+            half, start = divmod(tiles * part, 4)
             nc.vector.tensor_tensor(
-                out=g[:, 4 * half : 4 * half + 4, q, :, 64 * c4 : 64 * c4 + 64],
-                in0=accs[2 * pr, half][:].rearrange("p (i u w) -> p i u w", i=4, u=2),
-                in1=sgs[pr, half][:].rearrange("p (i u w) -> p i u w", i=4, u=2),
+                out=g[:, tiles * part : tiles * part + tiles, q, :, 64 * c4 : 64 * c4 + 64],
+                in0=accs[2 * pr, half][:, P * start : P * start + P * tiles].rearrange("p (i u w) -> p i u w", i=tiles, u=2),
+                in1=sgs[pr, part][:].rearrange("p (i u w) -> p i u w", i=tiles, u=2),
                 op=MULT,
             )
 
@@ -233,21 +263,21 @@ def tile_sanamixffndepthwiseglu_d1p_kernel(tc, x_bytes, x_scale, w1_words, w1_sc
         gg = {}
 
         def g_turn(q, m):
-            t = psum.tile([P, 2, 2, P], F32, name="gt_%d_%d" % (q, m), tag="tp", bufs=1)
+            t = psum.tile([P, 2, 2, P], F32, name="gt_%d_%d" % (q, m), tag="tp" if q == 0 else "h%d" % (m % 2), bufs=1)
             gt[q, m] = t
             for i2 in range(2):
                 for u in range(2):
                     nc.tensor.transpose(t[:, i2, u, :], g[:, 2 * m + i2, q, u, :].bitcast(F32), identf[:])
 
-        def g_copy(q, m):
-            gg[q, m] = turn_copy(gt[q, m], "gg_%d_%d" % (q, m))
+        def g_copy(q, m, vector=True):
+            gg[q, m] = turn_copy(gt[q, m], "gg_%d_%d" % (q, m), vector)
 
         def g_quant(q, m):
             cols = slice(256 * m, 256 * m + 256)
             nc.vector.quantize_mx(out=gq[:, q, cols].bitcast(FP8X4), scales=gqs[:, q, cols], in_=gg[q, m][:])
 
         outs = {}
-        out_tags = [("h0", 1), ("h1", 1), ("acc", 5), ("acc", 5)]
+        out_tags = [("acc", 5), ("acc", 5), ("tp", 1), ("acc", 5)]
 
         def mx2(i):
             tag, bufs = out_tags[i % 4]
@@ -307,60 +337,83 @@ def tile_sanamixffndepthwiseglu_d1p_kernel(tc, x_bytes, x_scale, w1_words, w1_sc
         mx1(1, 0)
         mx1(1, 1)
 
-        for n in range(17):
-            late = n - 2
-            if late >= 1 and late % 2 == 1:
-                gate_silu(late // 2, 1)
-                gate_mul(late // 2, 1)
-            if 10 <= n <= 13:
-                g_copy(0, n - 10)
-                g_quant(0, n - 10)
-            if n < 16:
-                alloc_units(n)
-                s_product(n, 0)
-            if n < 15:
-                silu1(n + 1, 0)
-                silu1(n + 1, 1)
+        for n in range(16):
+            pr = n // 2 - 1
+            gate = n % 2 == 1 and pr >= 0
+            alloc_units(n)
             if n >= 1:
                 gather(n - 1, 0)
+            if n < 15:
+                silu1(n + 1, 0)
+            if gate:
+                gate_silu(pr, 0)
+            if n < 15:
+                s_product(n, 0)
+                silu1(n + 1, 1)
             if n < 14:
                 mx1(n + 2, 0)
-                mx1(n + 2, 1)
-            if n < 16:
-                s_product(n, 1)
-                v_products(n)
-            if n >= 1 and (n - 1) % 2 == 1:
-                gate_silu((n - 1) // 2, 0)
-                gate_mul((n - 1) // 2, 0)
+            extra = []
+            if gate:
+                if n < 15:
+                    gate_silu(pr, 1)
+                extra = [(1, lambda: gate_mul(pr, 0)), (3, lambda: gate_mul(pr, 1))]
+            if 10 <= n <= 13:
+                g_copy(0, n - 10, VCOPY)
+            if n < 15:
+                v_products(n, 0, 32, extra)
+                for k in range(1, 5):
+                    s_product(n, k)
+            else:
+                for k in range(3):
+                    s_product(n, k, 0, 16)
+                gate_silu(pr, 1)
+                v_products(n, 0, 16, extra)
+                for k in range(3, 6):
+                    s_product(n, k, 0, 16)
+                for k in range(6):
+                    s_product(n, k, 16, 32)
+                v_products(n, 16, 32)
             if n >= 1:
                 gather(n - 1, 1)
-            if n < 16:
-                s_product(n, 2)
+            if n < 14:
+                if DUMMY:
+                    dummy(n + 2)
+                mx1(n + 2, 1)
+            if 10 <= n <= 13:
+                g_quant(0, n - 10)
             if 9 <= n <= 12:
                 g_turn(0, n - 9)
 
-        g_turn(1, 0)
-        g_copy(1, 0)
-        g_quant(1, 0)
-        gate_silu(7, 1)
-        gate_mul(7, 1)
+        for m in range(4):
+            gather(15, m, 4)
+            gate_silu(7, m, 4)
+            gate_mul(7, m, 4)
+            if m == 2:
+                g_turn(1, 0)
+                g_copy(1, 0, False)
+                g_quant(1, 0)
         g_turn(1, 1)
-        g_copy(1, 1)
-        g_quant(1, 1)
+        g_copy(1, 1, True)
         mx2(0)
         mx2(1)
-        g_turn(1, 2)
-        g_copy(1, 2)
-        g_quant(1, 2)
+        g_quant(1, 1)
         store(0)
+        g_turn(1, 2)
+        g_copy(1, 2, False)
         store(1)
+        g_quant(1, 2)
         mx2(2)
         mx2(3)
         g_turn(1, 3)
-        g_copy(1, 3)
+        g_copy(1, 3, True)
+        store(2)
         g_quant(1, 3)
-        for i in range(4, 8):
-            mx2(i)
-            store(i - 2)
+        store(3)
+        mx2(4)
+        mx2(5)
+        store(4)
+        store(5)
+        mx2(6)
+        mx2(7)
         store(6)
         store(7)

@@ -21,16 +21,18 @@ D = 512
 F = 1024
 FLOPS = 2 * T * D * 2 * F + 2 * T * F * D + 2 * 9 * T * 2 * F
 
-PLAN = [(3, 2), (4, 2)] * 8
-DUMMY = True
+PLAN = [(2, 2), (2, 4), (3, 3), (4, 0), (3, 3), (4, 0), (3, 3), (4, 0), (3, 2), (4, 0), (4, 2), (4, 0), (5, 1), (5, 0), (5, 0), (3, 0)]
 VCOPY = True
+TAPS = [1, 4, 7, 0, 2, 3, 5, 6, 8]
+SETS = 4
+UNITS = 7
 
 
 def split_taps(s, v):
-    lists = [[s + k] for k in range(v)]
-    for k, tap in enumerate(range(s + v, 9)):
-        lists[k % v].append(tap)
-    return list(range(s)), lists
+    lists = [[TAPS[k]] for k in range(s + v)]
+    for k, tap in enumerate(TAPS[s + v :]):
+        lists[k % 3].append(tap)
+    return lists
 
 
 def tile_sanamixffndepthwiseglu_d1p_kernel(tc, x_bytes, x_scale, w1_words, w1_scales, b1, wd, gain, w2_words, w2_scales, out):
@@ -58,10 +60,13 @@ def tile_sanamixffndepthwiseglu_d1p_kernel(tc, x_bytes, x_scale, w1_words, w1_sc
         xw = const.tile([P, 8, D], BF16, name="xw", align_bytes=64)
         xq = const.tile([P, T], U32, name="xq", align_bytes=64)
         xqs = const.tile([P, T], U8, name="xqs", align_bytes=64)
-        u0 = const.tile([P, 34, 34], F32, name="u0", align_bytes=64)
-        u1 = const.tile([P, 34, 34], F32, name="u1", align_bytes=64)
-        u2 = const.tile([P, 34, 34], F32, name="u2", align_bytes=64)
-        us = [u0, u1, u2]
+        us = []
+        for k in range(4):
+            us.append(const.tile([P, 34, 32], F32, name="u%d" % k, align_bytes=64))
+        unit_sets = []
+        most = max(s + v for s, v in PLAN)
+        for k in range(SETS):
+            unit_sets.append([const.tile([P, T], F32, name="unit_%d_%d" % (k, j), align_bytes=64) for j in range(most)])
         g = const.tile([P, 8, 2, 2, 256], BF16, name="g", align_bytes=64)
         gq = const.tile([P, 2, T], U32, name="gq", align_bytes=64)
         gqs = const.tile([P, 2, T], U8, name="gqs", align_bytes=64)
@@ -94,10 +99,14 @@ def tile_sanamixffndepthwiseglu_d1p_kernel(tc, x_bytes, x_scale, w1_words, w1_sc
             )
 
         make_identity(nc, identf[:])
-        nc.gpsimd.memset(u0[:], 0.0)
         make_identity(nc, identb[:])
-        nc.gpsimd.memset(u1[:], 0.0)
-        nc.gpsimd.memset(u2[:], 0.0)
+        for k in range(4):
+            nc.gpsimd.memset(us[k][:, 0, :], 0.0)
+            nc.gpsimd.memset(us[k][:, 33, :], 0.0)
+        for k in range(SETS):
+            for j in range(3, most):
+                edge = {0: 0, 1: 31}.get((j - 3) % 2, 0)
+                nc.vector.memset(unit_sets[k][j][:].rearrange("p (r w) -> p r w", w=32)[:, :, edge : edge + 1], 0.0)
 
         def widen(m):
             for i in (2 * m, 2 * m + 1):
@@ -168,13 +177,15 @@ def tile_sanamixffndepthwiseglu_d1p_kernel(tc, x_bytes, x_scale, w1_words, w1_sc
         def silu1(n, half):
             c = order[n]
             nc.scalar.activation(
-                out=us[n % 3][:, 1 + 16 * half : 17 + 16 * half, 1:33],
+                out=us[n % 4][:, 1 + 16 * half : 17 + 16 * half, :],
                 in_=hs[n, half][:].rearrange("p (r w) -> p r w", w=32),
                 func=ACT.Silu,
                 bias=par[:, 144 + c : 145 + c],
             )
 
         units = {}
+        for n in range(16):
+            units[n] = unit_sets[n % SETS][: PLAN[n][0] + PLAN[n][1]]
 
         def tap_weight(n, tap):
             c = order[n]
@@ -182,45 +193,36 @@ def tile_sanamixffndepthwiseglu_d1p_kernel(tc, x_bytes, x_scale, w1_words, w1_sc
                 return wg[:, tap, c : c + 1]
             return par[:, 16 * tap + c : 16 * tap + c + 1]
 
-        def window(n, tap, lo, hi):
+        def tap_views(n, k, tap, lo, hi):
             r, t = divmod(tap, 3)
-            return us[n % 3][:, r + lo : r + hi, t : t + 32]
-
-        def new_unit(n, k):
-            t = work.tile([P, T], F32, name="unit_%d_%d" % (n, k), tag="unit%d" % k, bufs=3, align_bytes=64)
-            units[n].append(t)
-            return t
-
-        def rows(t, lo, hi):
-            return t[:, 32 * lo : 32 * hi].rearrange("p (r w) -> p r w", w=32)
-
-        def spec(n):
-            return split_taps(PLAN[n][0], PLAN[n][1])
-
-        def alloc_units(n):
-            units[n] = []
-            s, v = spec(n)
-            for k in range(len(s) + len(v)):
-                new_unit(n, k)
+            src = us[n % 4]
+            dst = units[n][k][:, 32 * lo : 32 * hi].rearrange("p (r w) -> p r w", w=32)
+            if t == 0:
+                return src[:, r + lo : r + hi, 0:31], dst[:, :, 1:32]
+            if t == 1:
+                return src[:, r + lo : r + hi, :], dst
+            return src[:, r + lo : r + hi, 1:32], dst[:, :, 0:31]
 
         def s_product(n, k, lo=0, hi=32):
-            if k < len(spec(n)[0]):
-                tap = spec(n)[0][k]
-                nc.scalar.activation(out=rows(units[n][k], lo, hi), in_=window(n, tap, lo, hi), func=ACT.Copy, scale=tap_weight(n, tap))
+            if k < PLAN[n][0]:
+                tap = TAPS[k]
+                src, dst = tap_views(n, k, tap, lo, hi)
+                nc.scalar.activation(out=dst, in_=src, func=ACT.Copy, scale=tap_weight(n, tap))
 
         def v_products(n, lo, hi, extra=()):
-            s, v = spec(n)
-            work_list = []
-            for d in range(max(len(taps) for taps in v)):
-                for k, taps in enumerate(v):
+            s, v = PLAN[n]
+            lists = split_taps(s, v)
+            work_list = [(k, 0, lists[k][0]) for k in range(s, s + v)]
+            for d in range(1, max(len(taps) for taps in lists)):
+                for k, taps in enumerate(lists):
                     if d < len(taps):
                         work_list.append((k, d, taps[d]))
             for pos, (k, d, tap) in enumerate(work_list):
-                unit = rows(units[n][len(s) + k], lo, hi)
+                src, dst = tap_views(n, k, tap, lo, hi)
                 if d == 0:
-                    nc.vector.tensor_scalar(out=unit, in0=window(n, tap, lo, hi), scalar1=tap_weight(n, tap), scalar2=None, op0=MULT)
+                    nc.vector.tensor_scalar(out=dst, in0=src, scalar1=tap_weight(n, tap), scalar2=None, op0=MULT)
                 else:
-                    nc.vector.scalar_tensor_tensor(out=unit, in0=window(n, tap, lo, hi), scalar=tap_weight(n, tap), in1=unit, op0=MULT, op1=ADD)
+                    nc.vector.scalar_tensor_tensor(out=dst, in0=src, scalar=tap_weight(n, tap), in1=dst, op0=MULT, op1=ADD)
                 for at, fn in extra:
                     if at == pos:
                         fn()
@@ -336,67 +338,69 @@ def tile_sanamixffndepthwiseglu_d1p_kernel(tc, x_bytes, x_scale, w1_words, w1_sc
         silu1(0, 1)
         mx1(1, 0)
         mx1(1, 1)
+        s_product(0, 0)
+        silu1(1, 0)
+        mx1(2, 0)
+        s_product(0, 1)
+        silu1(1, 1)
+        mx1(2, 1)
+        for k in range(2, 6):
+            s_product(0, k)
 
         for n in range(16):
             pr = n // 2 - 1
             gate = n % 2 == 1 and pr >= 0
-            alloc_units(n)
+            extra = []
             if n >= 1:
                 gather(n - 1, 0)
             if n < 15:
-                silu1(n + 1, 0)
+                s_product(n + 1, 0)
+            if n < 14:
+                silu1(n + 2, 0)
             if gate:
                 gate_silu(pr, 0)
-            if n < 15:
-                s_product(n, 0)
-                silu1(n + 1, 1)
-            if n < 14:
-                mx1(n + 2, 0)
-            extra = []
-            if gate:
-                if n < 15:
-                    gate_silu(pr, 1)
                 extra = [(1, lambda: gate_mul(pr, 0)), (3, lambda: gate_mul(pr, 1))]
+            if n < 13:
+                mx1(n + 3, 0)
+            if n < 15:
+                s_product(n + 1, 1)
+            if n < 14:
+                silu1(n + 2, 1)
+            if gate:
+                gate_silu(pr, 1)
+            if n < 15:
+                for k in range(2, 6):
+                    s_product(n + 1, k)
             if 10 <= n <= 13:
                 g_copy(0, n - 10, VCOPY)
-            if n < 15:
-                v_products(n, 0, 32, extra)
-                for k in range(1, 5):
-                    s_product(n, k)
-            else:
-                for k in range(3):
-                    s_product(n, k, 0, 16)
-                gate_silu(pr, 1)
-                v_products(n, 0, 16, extra)
-                for k in range(3, 6):
-                    s_product(n, k, 0, 16)
-                for k in range(6):
-                    s_product(n, k, 16, 32)
-                v_products(n, 16, 32)
+            v_products(n, 0, 32 if n < 15 else 16, extra)
             if n >= 1:
                 gather(n - 1, 1)
-            if n < 14:
-                if DUMMY:
-                    dummy(n + 2)
-                mx1(n + 2, 1)
+            if n < 13:
+                mx1(n + 3, 1)
             if 10 <= n <= 13:
                 g_quant(0, n - 10)
             if 9 <= n <= 12:
                 g_turn(0, n - 9)
-
-        for m in range(4):
+        for m in range(2):
             gather(15, m, 4)
             gate_silu(7, m, 4)
-            gate_mul(7, m, 4)
-            if m == 2:
-                g_turn(1, 0)
-                g_copy(1, 0, False)
-                g_quant(1, 0)
+        v_products(15, 16, 32, [(1, lambda: gate_mul(7, 0, 4)), (2, lambda: gate_mul(7, 1, 4))])
+
+        g_turn(1, 0)
+        g_copy(1, 0, False)
         g_turn(1, 1)
-        g_copy(1, 1, True)
+        g_copy(1, 1, False)
+        gather(15, 2, 4)
+        g_quant(1, 0)
+        gate_silu(7, 2, 4)
         mx2(0)
         mx2(1)
+        gather(15, 3, 4)
+        gate_mul(7, 2, 4)
+        gate_silu(7, 3, 4)
         g_quant(1, 1)
+        gate_mul(7, 3, 4)
         store(0)
         g_turn(1, 2)
         g_copy(1, 2, False)

@@ -21,9 +21,19 @@ D = 512
 F = 1024
 FLOPS = 2 * T * D * 2 * F + 2 * T * F * D + 2 * 9 * T * 2 * F
 
-PLAN = [(2, 2), (2, 4), (3, 3), (4, 0), (3, 3), (4, 0), (3, 3), (4, 0), (3, 2), (4, 0), (4, 2), (4, 0), (5, 1), (5, 0), (5, 0), (3, 0)]
+PLAN = [(3, 3), (3, 2), (3, 3), (4, 2), (3, 3), (4, 2), (2, 2), (4, 2), (3, 3), (4, 2), (3, 3), (4, 2), (3, 3), (4, 2), (3, 3), (3, 0)]
 VCOPY = True
+KEEP_0 = 0
+KEEP_1 = 0
+KEEP_A = 2
+LATE_KEEP = 2
+G0 = 3
+G1 = 4
+HEAD_KEEP = 4
 TAPS = [1, 4, 7, 0, 2, 3, 5, 6, 8]
+ROW = 36
+LEFT = 4
+FLAT = 1232
 SETS = 4
 UNITS = 7
 
@@ -31,7 +41,7 @@ UNITS = 7
 def split_taps(s, v):
     lists = [[TAPS[k]] for k in range(s + v)]
     for k, tap in enumerate(TAPS[s + v :]):
-        lists[k % 3].append(tap)
+        lists[s + k % v if v else k % s].append(tap)
     return lists
 
 
@@ -62,7 +72,7 @@ def tile_sanamixffndepthwiseglu_d1p_kernel(tc, x_bytes, x_scale, w1_words, w1_sc
         xqs = const.tile([P, T], U8, name="xqs", align_bytes=64)
         us = []
         for k in range(4):
-            us.append(const.tile([P, 34, 32], F32, name="u%d" % k, align_bytes=64))
+            us.append(const.tile([P, FLAT], F32, name="u%d" % k, align_bytes=64))
         unit_sets = []
         most = max(s + v for s, v in PLAN)
         for k in range(SETS):
@@ -101,12 +111,7 @@ def tile_sanamixffndepthwiseglu_d1p_kernel(tc, x_bytes, x_scale, w1_words, w1_sc
         make_identity(nc, identf[:])
         make_identity(nc, identb[:])
         for k in range(4):
-            nc.gpsimd.memset(us[k][:, 0, :], 0.0)
-            nc.gpsimd.memset(us[k][:, 33, :], 0.0)
-        for k in range(SETS):
-            for j in range(3, most):
-                edge = {0: 0, 1: 31}.get((j - 3) % 2, 0)
-                nc.vector.memset(unit_sets[k][j][:].rearrange("p (r w) -> p r w", w=32)[:, :, edge : edge + 1], 0.0)
+            nc.gpsimd.memset(us[k][:], 0.0)
 
         def widen(m):
             for i in (2 * m, 2 * m + 1):
@@ -121,7 +126,7 @@ def tile_sanamixffndepthwiseglu_d1p_kernel(tc, x_bytes, x_scale, w1_words, w1_sc
         xg = {}
 
         def x_turn(m):
-            t = psum.tile([P, 2, 2, P], F32, name="xt_%d" % m, tag="acc", bufs=5)
+            t = psum.tile([P, 2, 2, P], F32, name="xt_%d" % m, tag="b%d" % m, bufs=1)
             xt[m] = t
             for i2 in range(2):
                 words = xw[:, 2 * m + i2, :].bitcast(F32)
@@ -154,14 +159,11 @@ def tile_sanamixffndepthwiseglu_d1p_kernel(tc, x_bytes, x_scale, w1_words, w1_sc
         def h_tile(n, half):
             hs[n, half] = psum.tile([P, 512], F32, name="h_%d_%d" % (n, half), tag="h%d" % half, bufs=1)
 
-        def dummy(n):
-            h_tile(n, 1)
-            nc.tensor.matmul(hs[n, 1][:], lhsT=identb[:], rhs=xw[:, 0, :], start=True, stop=True)
-
-        def mx1(n, half):
+        def mx1(n, half, keep=0):
             c = order[n]
-            if (n, half) not in hs:
-                h_tile(n, half)
+            h_tile(n, half)
+            for j in range(keep):
+                keep_clock(hs[n, half], j)
             h = hs[n, half]
             cols = slice(512 * half, 512 * half + 512)
             nc.tensor.matmul_mx(
@@ -174,10 +176,13 @@ def tile_sanamixffndepthwiseglu_d1p_kernel(tc, x_bytes, x_scale, w1_words, w1_sc
                 stop=True,
             )
 
+        def u_rows(n, base, count):
+            return us[n % 4][:, base : base + ROW * count].rearrange("p (r w) -> p r w", w=ROW)[:, :, 0:32]
+
         def silu1(n, half):
             c = order[n]
             nc.scalar.activation(
-                out=us[n % 4][:, 1 + 16 * half : 17 + 16 * half, :],
+                out=u_rows(n, (1 + 16 * half) * ROW + LEFT, 16),
                 in_=hs[n, half][:].rearrange("p (r w) -> p r w", w=32),
                 func=ACT.Silu,
                 bias=par[:, 144 + c : 145 + c],
@@ -195,13 +200,8 @@ def tile_sanamixffndepthwiseglu_d1p_kernel(tc, x_bytes, x_scale, w1_words, w1_sc
 
         def tap_views(n, k, tap, lo, hi):
             r, t = divmod(tap, 3)
-            src = us[n % 4]
             dst = units[n][k][:, 32 * lo : 32 * hi].rearrange("p (r w) -> p r w", w=32)
-            if t == 0:
-                return src[:, r + lo : r + hi, 0:31], dst[:, :, 1:32]
-            if t == 1:
-                return src[:, r + lo : r + hi, :], dst
-            return src[:, r + lo : r + hi, 1:32], dst[:, :, 0:31]
+            return u_rows(n, (r + lo) * ROW + LEFT - 1 + t, hi - lo), dst
 
         def s_product(n, k, lo=0, hi=32):
             if k < PLAN[n][0]:
@@ -224,23 +224,33 @@ def tile_sanamixffndepthwiseglu_d1p_kernel(tc, x_bytes, x_scale, w1_words, w1_sc
                 else:
                     nc.vector.scalar_tensor_tensor(out=dst, in0=src, scalar=tap_weight(n, tap), in1=dst, op0=MULT, op1=ADD)
                 for at, fn in extra:
-                    if at == pos:
+                    if min(at, len(work_list) - 1) == pos:
                         fn()
 
         accs = {}
 
-        def gather(n, part, parts=2):
-            tiles = 8 // parts
-            acc = psum.tile([P, P * tiles], F32, name="acc_%d_%d" % (n, part), tag="acc", bufs=5)
-            accs[n, part] = acc
+        def acc_tile(n, part, parts):
+            bank = (2 * n + part) % 5 if parts == 2 else part
+            accs[n, part] = psum.tile([P, T // parts], F32, name="acc_%d_%d" % (n, part), tag="b%d" % bank, bufs=1)
+
+        def gather_tile(n, part, j, parts=2):
+            if j == 0:
+                acc_tile(n, part, parts)
+            acc = accs[n, part]
+            lo = T // parts * part + P * j
             count = len(units[n])
-            for j in range(tiles):
-                lo = P * (tiles * part + j)
-                for k in range(count):
-                    nc.tensor.matmul(
-                        acc[:, P * j : P * j + P], lhsT=units[n][k][:, lo : lo + P], rhs=perm[:],
-                        start=(k == 0), stop=(k == count - 1), is_transpose=True,
-                    )
+            for k in range(count):
+                nc.tensor.matmul(
+                    acc[:, P * j : P * j + P], lhsT=units[n][k][:, lo : lo + P], rhs=perm[:],
+                    start=(k == 0), stop=(k == count - 1), is_transpose=True,
+                )
+
+        def gather(n, part, parts=2):
+            for j in range(8 // parts):
+                gather_tile(n, part, j, parts)
+
+        def keep_clock(bank, j):
+            nc.tensor.matmul(bank[:, P * j : P * j + P], lhsT=identf[:], rhs=identf[:], start=True, stop=True)
 
         sgs = {}
 
@@ -265,7 +275,7 @@ def tile_sanamixffndepthwiseglu_d1p_kernel(tc, x_bytes, x_scale, w1_words, w1_sc
         gg = {}
 
         def g_turn(q, m):
-            t = psum.tile([P, 2, 2, P], F32, name="gt_%d_%d" % (q, m), tag="tp" if q == 0 else "h%d" % (m % 2), bufs=1)
+            t = psum.tile([P, 2, 2, P], F32, name="gt_%d_%d" % (q, m), tag="tp" if q == 0 else ("h0", "h1", "tp", "h0")[m], bufs=1)
             gt[q, m] = t
             for i2 in range(2):
                 for u in range(2):
@@ -279,23 +289,21 @@ def tile_sanamixffndepthwiseglu_d1p_kernel(tc, x_bytes, x_scale, w1_words, w1_sc
             nc.vector.quantize_mx(out=gq[:, q, cols].bitcast(FP8X4), scales=gqs[:, q, cols], in_=gg[q, m][:])
 
         outs = {}
-        out_tags = [("acc", 5), ("acc", 5), ("tp", 1), ("acc", 5)]
+        out_tags = ("b0", "b1", "h1", "b2", "b3", "b4", "b0", "b1")
 
-        def mx2(i):
-            tag, bufs = out_tags[i % 4]
-            o = psum.tile([P, D], F32, name="o_%d" % i, tag=tag, bufs=bufs)
-            outs[i] = o
+        def mx2(i, q):
+            if q == 0:
+                outs[i] = psum.tile([P, D], F32, name="o_%d" % i, tag=out_tags[i], bufs=1)
             tok = slice(P * i, P * i + P)
-            for q in range(2):
-                nc.tensor.matmul_mx(
-                    out=o[:],
-                    lhsT=gq[:, q, tok].bitcast(FP8X4),
-                    lhsT_scale=gqs[:, q, tok],
-                    rhs=w2[:, q, :].bitcast(FP4X4),
-                    rhs_scale=w2s[:, q, :],
-                    start=(q == 0),
-                    stop=(q == 1),
-                )
+            nc.tensor.matmul_mx(
+                out=outs[i][:],
+                lhsT=gq[:, q, tok].bitcast(FP8X4),
+                lhsT_scale=gqs[:, q, tok],
+                rhs=w2[:, q, :].bitcast(FP4X4),
+                rhs_scale=w2s[:, q, :],
+                start=(q == 0),
+                stop=(q == 1),
+            )
 
         def store(i):
             ob = work.tile([P, D], F32, name="ob_%d" % i, tag="ob", bufs=8, align_bytes=64)
@@ -305,6 +313,9 @@ def tile_sanamixffndepthwiseglu_d1p_kernel(tc, x_bytes, x_scale, w1_words, w1_sc
                 nc.vector.tensor_copy(out=ob[:], in_=outs[i][:])
             nc.sync.dma_start(out=ov[P * i : P * i + P, :], in_=ob[:])
 
+        spare = psum.tile([P, 512], F32, name="spare", tag="b4", bufs=1)
+        for k in range(HEAD_KEEP):
+            keep_clock(spare, k % 4)
         widen(0)
         widen(1)
         x_turn(0)
@@ -338,86 +349,92 @@ def tile_sanamixffndepthwiseglu_d1p_kernel(tc, x_bytes, x_scale, w1_words, w1_sc
         silu1(0, 1)
         mx1(1, 0)
         mx1(1, 1)
-        s_product(0, 0)
-        silu1(1, 0)
-        mx1(2, 0)
-        s_product(0, 1)
-        silu1(1, 1)
-        mx1(2, 1)
-        for k in range(2, 6):
-            s_product(0, k)
 
         for n in range(16):
             pr = n // 2 - 1
             gate = n % 2 == 1 and pr >= 0
             extra = []
             if n >= 1:
-                gather(n - 1, 0)
+                gather_tile(n - 1, 0, 0)
+                gather_tile(n - 1, 0, 1)
+                for j in range(KEEP_A):
+                    keep_clock(accs[n - 1, 0], 2 + j)
+                gather_tile(n - 1, 0, 2)
+                gather_tile(n - 1, 0, 3)
             if n < 15:
-                s_product(n + 1, 0)
-            if n < 14:
-                silu1(n + 2, 0)
+                silu1(n + 1, 0)
             if gate:
                 gate_silu(pr, 0)
                 extra = [(1, lambda: gate_mul(pr, 0)), (3, lambda: gate_mul(pr, 1))]
-            if n < 13:
-                mx1(n + 3, 0)
             if n < 15:
-                s_product(n + 1, 1)
-            if n < 14:
-                silu1(n + 2, 1)
-            if gate:
+                s_product(n, 0)
+                silu1(n + 1, 1)
+                if gate:
+                    gate_silu(pr, 1)
+                for k in range(1, 6):
+                    s_product(n, k)
+            else:
+                for k in range(3):
+                    s_product(n, k, 0, 16)
                 gate_silu(pr, 1)
-            if n < 15:
-                for k in range(2, 6):
-                    s_product(n + 1, k)
+                for k in range(3, 6):
+                    s_product(n, k, 0, 16)
+                for k in range(6):
+                    s_product(n, k, 16, 32)
+            v_products(n, 0, 32 if n < 15 else 16, extra)
             if 10 <= n <= 13:
                 g_copy(0, n - 10, VCOPY)
-            v_products(n, 0, 32 if n < 15 else 16, extra)
             if n >= 1:
-                gather(n - 1, 1)
-            if n < 13:
-                mx1(n + 3, 1)
-            if 10 <= n <= 13:
-                g_quant(0, n - 10)
+                gather_tile(n - 1, 1, 0)
+            if n < 14:
+                mx1(n + 2, 0, KEEP_0)
+            else:
+                for j in range(LATE_KEEP):
+                    keep_clock(accs[n - 1, 1], 1 + j)
+            if n >= 1:
+                for j in range(1, 4):
+                    gather_tile(n - 1, 1, j)
+            if n < 14:
+                mx1(n + 2, 1, KEEP_1)
+            if 11 <= n <= 14:
+                g_quant(0, n - 11)
             if 9 <= n <= 12:
                 g_turn(0, n - 9)
         for m in range(2):
             gather(15, m, 4)
             gate_silu(7, m, 4)
-        v_products(15, 16, 32, [(1, lambda: gate_mul(7, 0, 4)), (2, lambda: gate_mul(7, 1, 4))])
+        v_products(15, 16, 32, [(G0, lambda: gate_mul(7, 0, 4)), (G1, lambda: gate_mul(7, 1, 4))])
 
         g_turn(1, 0)
         g_copy(1, 0, False)
         g_turn(1, 1)
         g_copy(1, 1, False)
         gather(15, 2, 4)
-        g_quant(1, 0)
         gate_silu(7, 2, 4)
-        mx2(0)
-        mx2(1)
         gather(15, 3, 4)
-        gate_mul(7, 2, 4)
         gate_silu(7, 3, 4)
+        g_quant(1, 0)
+        gate_mul(7, 2, 4)
         g_quant(1, 1)
         gate_mul(7, 3, 4)
+        for i in range(2):
+            mx2(i, 0)
+            mx2(i, 1)
         store(0)
         g_turn(1, 2)
-        g_copy(1, 2, False)
-        store(1)
-        g_quant(1, 2)
-        mx2(2)
-        mx2(3)
         g_turn(1, 3)
+        g_copy(1, 2, False)
         g_copy(1, 3, True)
+        store(1)
+        for i in (2, 3):
+            mx2(i, 0)
+            mx2(i, 1)
+        g_quant(1, 2)
         store(2)
         g_quant(1, 3)
         store(3)
-        mx2(4)
-        mx2(5)
-        store(4)
-        store(5)
-        mx2(6)
-        mx2(7)
-        store(6)
-        store(7)
+        for i in range(4, 8):
+            mx2(i, 0)
+        for i in range(4, 8):
+            mx2(i, 1)
+            store(i)

@@ -21,16 +21,16 @@ D = 512
 F = 1024
 FLOPS = 2 * T * D * 2 * F + 2 * T * F * D + 2 * 9 * T * 2 * F
 
-PLAN = [(3, 3), (3, 2), (3, 3), (4, 2), (3, 3), (4, 2), (2, 2), (4, 2), (3, 3), (4, 2), (3, 3), (4, 2), (3, 3), (4, 2), (3, 3), (3, 0)]
+PLAN = [(4, 1), (3, 3), (3, 3), (4, 3), (3, 3), (5, 1), (2, 3), (4, 2), (3, 3), (4, 2), (3, 3), (5, 2), (3, 3), (3, 3), (3, 4), (3, 0)]
 VCOPY = True
 KEEP_0 = 0
 KEEP_1 = 0
 KEEP_A = 2
-LATE_KEEP = 2
+LATE_KEEP = 1
 G0 = 3
 G1 = 4
-HEAD_KEEP = 4
-TAPS = [1, 4, 7, 0, 2, 3, 5, 6, 8]
+HEAD_KEEP = 5
+TAPS = [0, 2, 3, 5, 6, 8, 1, 4, 7]
 ROW = 36
 LEFT = 4
 FLAT = 1232
@@ -81,26 +81,26 @@ def tile_sanamixffndepthwiseglu_d1p_kernel(tc, x_bytes, x_scale, w1_words, w1_sc
         gq = const.tile([P, 2, T], U32, name="gq", align_bytes=64)
         gqs = const.tile([P, 2, T], U8, name="gqs", align_bytes=64)
 
-        xv = x_bytes.rearrange("o a b k -> (o a b) k").rearrange("(i p) k -> p i k", p=P)
-        xsv = x_scale.rearrange("o a b j -> (o a b) j").rearrange("(i p) j -> p i j", p=P)
+        xv = x_bytes.rearrange("o a b k -> (o a b) k").rearrange("(p i) k -> p i k", i=8)
+        xsv = x_scale.rearrange("o a b j -> (o a b) j").rearrange("(p i) j -> p i j", i=8)
         ov = out.rearrange("o a b n -> (o a b) n")
         wdv = wd.rearrange("r t (c p) -> (r t c) p", p=P)
 
         nc.scalar.dma_start(out=xs[:], in_=xsv)
-        for m in range(4):
-            nc.sync.dma_start(out=xb[:, 2 * m : 2 * m + 2, :], in_=xv[:, 2 * m : 2 * m + 2, :])
-        nc.vector.memset(warm[:], 0.0)
-        nc.vector.memset(prm_b[:], 0.0)
         nc.vector.memset(w1s[:].bitcast(I32), 0)
-        nc.vector.memset(w2s[:].rearrange("p g n -> p (g n)").bitcast(I32), 0)
-        nc.scalar.dma_start(out=prm_a[:], in_=wdv[0:P, :])
-        nc.scalar.dma_start(out=prm_b[0:16, :], in_=wdv[P : P + 16, :])
-        nc.scalar.dma_start(out=prm_b[16:32, :], in_=b1.rearrange("(c p) -> c p", p=P))
-        nc.scalar.dma_start(out=prm_b[32:40, :], in_=gain.rearrange("(c p) -> c p", p=P))
+        nc.vector.memset(warm[:], 0.0)
         nc.scalar.activation(out=warm[:], in_=warm[:], func=ACT.Silu)
+        for m in range(2):
+            nc.sync.dma_start(out=xb[:, 4 * m : 4 * m + 4, :], in_=xv[:, 4 * m : 4 * m + 4, :])
         nc.sync.dma_start(out=w1[:].bitcast(I32), in_=w1_words[0].bitcast(I32))
         for q in range(4):
             nc.sync.dma_start(out=w1s[32 * q : 32 * q + 4, :].bitcast(I32), in_=w1_scales[0, 4 * q : 4 * q + 4, :].bitcast(I32))
+        nc.vector.memset(prm_b[:], 0.0)
+        nc.sync.dma_start(out=prm_a[:], in_=wdv[0:P, :])
+        nc.sync.dma_start(out=prm_b[0:16, :], in_=wdv[P : P + 16, :])
+        nc.sync.dma_start(out=prm_b[16:32, :], in_=b1.rearrange("(c p) -> c p", p=P))
+        nc.sync.dma_start(out=prm_b[32:40, :], in_=gain.rearrange("(c p) -> c p", p=P))
+        nc.vector.memset(w2s[:].rearrange("p g n -> p (g n)").bitcast(I32), 0)
         nc.sync.dma_start(out=w2[:].rearrange("p g n -> p (g n)").bitcast(I32).rearrange("p (g n) -> p g n", g=2), in_=w2_words.bitcast(I32).rearrange("g p n -> p g n"))
         for q in range(4):
             nc.sync.dma_start(
@@ -111,7 +111,9 @@ def tile_sanamixffndepthwiseglu_d1p_kernel(tc, x_bytes, x_scale, w1_words, w1_sc
         make_identity(nc, identf[:])
         make_identity(nc, identb[:])
         for k in range(4):
-            nc.gpsimd.memset(us[k][:], 0.0)
+            nc.vector.memset(us[k][:, 0 : ROW], 0.0)
+            nc.vector.memset(us[k][:, ROW : 33 * ROW].rearrange("p (r w) -> p r w", w=ROW)[:, :, 0:LEFT], 0.0)
+            nc.vector.memset(us[k][:, 33 * ROW : FLAT], 0.0)
 
         def widen(m):
             for i in (2 * m, 2 * m + 1):
@@ -143,8 +145,8 @@ def tile_sanamixffndepthwiseglu_d1p_kernel(tc, x_bytes, x_scale, w1_words, w1_sc
                 nc.scalar.copy(out=o, in_=s)
             return dst
 
-        def x_copy(m):
-            xg[m] = turn_copy(xt[m], "xg_%d" % m)
+        def x_copy(m, vector=False):
+            xg[m] = turn_copy(xt[m], "xg_%d" % m, vector)
 
         def x_quant(m):
             cols = slice(256 * m, 256 * m + 256)
@@ -182,8 +184,8 @@ def tile_sanamixffndepthwiseglu_d1p_kernel(tc, x_bytes, x_scale, w1_words, w1_sc
         def silu1(n, half):
             c = order[n]
             nc.scalar.activation(
-                out=u_rows(n, (1 + 16 * half) * ROW + LEFT, 16),
-                in_=hs[n, half][:].rearrange("p (r w) -> p r w", w=32),
+                out=u_rows(n, ROW + LEFT, 32).rearrange("p a (b i) -> p a b i", i=8)[:, :, :, 4 * half : 4 * half + 4],
+                in_=hs[n, half][:].rearrange("p (i a b) -> p a b i", i=4, b=4),
                 func=ACT.Silu,
                 bias=par[:, 144 + c : 145 + c],
             )
@@ -316,26 +318,21 @@ def tile_sanamixffndepthwiseglu_d1p_kernel(tc, x_bytes, x_scale, w1_words, w1_sc
         spare = psum.tile([P, 512], F32, name="spare", tag="b4", bufs=1)
         for k in range(HEAD_KEEP):
             keep_clock(spare, k % 4)
-        widen(0)
-        widen(1)
-        x_turn(0)
-        x_turn(1)
-        x_copy(0)
-        widen(2)
-        x_quant(0)
-        x_turn(2)
-        x_copy(1)
-        widen(3)
-        x_quant(1)
-        x_turn(3)
-        x_copy(2)
+        nc.vector.tensor_copy(out=perm[:].rearrange("q (u p e) -> q u p e", u=2, e=2), in_=identf[:].rearrange("q (p u e) -> q u p e", u=2, e=2))
+        for m in range(4):
+            widen(m)
+            x_turn(m)
         pt = psum.tile([P, 2, P], BF16, name="pt", tag="tp", bufs=1)
         nc.tensor.transpose(pt[:, 0, :], prm_a[:], identb[:])
         nc.tensor.transpose(pt[:, 1, :], prm_b[:], identb[:])
-        nc.vector.tensor_copy(out=par[:], in_=pt[:].rearrange("p a b -> p (a b)")[:, 0:168])
+        for m in range(3):
+            x_copy(m)
+            x_quant(m)
+            if m == 1:
+                nc.vector.tensor_copy(out=par[:], in_=pt[:].rearrange("p a b -> p (a b)")[:, 0:168])
         mx1(0, 0)
         x_copy(3)
-        x_quant(2)
+        x_quant(3)
         nc.vector.tensor_tensor(
             out=wg[:],
             in0=par[:, 0:144].rearrange("p (k c) -> p k c", c=16)[:, :, 0:8],
@@ -343,8 +340,6 @@ def tile_sanamixffndepthwiseglu_d1p_kernel(tc, x_bytes, x_scale, w1_words, w1_sc
             op=MULT,
         )
         silu1(0, 0)
-        x_quant(3)
-        nc.vector.tensor_copy(out=perm[:].rearrange("q (u p e) -> q u p e", u=2, e=2), in_=identf[:].rearrange("q (p u e) -> q u p e", u=2, e=2))
         mx1(0, 1)
         silu1(0, 1)
         mx1(1, 0)

from contextlib import ExitStack

import concourse.mybir as mybir
from concourse.masks import make_identity

F32 = mybir.dt.float32
BF16 = mybir.dt.bfloat16
U8 = mybir.dt.uint8
U32 = mybir.dt.uint32
I32 = mybir.dt.int32
FP8 = mybir.dt.float8_e4m3fn
FP8X4 = mybir.dt.float8_e4m3fn_x4
FP4X4 = mybir.dt.float4_e2m1fn_x4
ACT = mybir.ActivationFunctionType
MULT = mybir.AluOpType.mult
ADD = mybir.AluOpType.add

P = 128
T = 1024
D = 512
F = 1024
FLOPS = 2 * T * D * 2 * F + 2 * T * F * D + 2 * 9 * T * 2 * F

PLAN = [(4, 1), (3, 3), (3, 3), (4, 3), (3, 3), (5, 1), (2, 3), (4, 2), (3, 3), (4, 2), (3, 3), (5, 2), (3, 3), (3, 3), (3, 4), (3, 0)]
VCOPY = True
KEEP_0 = 0
KEEP_1 = 0
KEEP_A = 2
LATE_KEEP = 1
G0 = 3
G1 = 4
HEAD_KEEP = 5
TAPS = [0, 2, 3, 5, 6, 8, 1, 4, 7]
ROW = 36
LEFT = 4
FLAT = 1232
SETS = 4
UNITS = 7


def split_taps(s, v):
    lists = [[TAPS[k]] for k in range(s + v)]
    for k, tap in enumerate(TAPS[s + v :]):
        lists[s + k % v if v else k % s].append(tap)
    return lists


def tile_sanamixffndepthwiseglu_d1p_kernel(tc, x_bytes, x_scale, w1_words, w1_scales, b1, wd, gain, w2_words, w2_scales, out):
    nc = tc.nc
    with ExitStack() as ctx:
        const = ctx.enter_context(tc.tile_pool(name="const", bufs=1))
        work = ctx.enter_context(tc.tile_pool(name="work", bufs=3))
        psum = ctx.enter_context(tc.psum_pool(name="psum", bufs=1))
        ctx.enter_context(tc.manual_schedule())

        xb = const.tile([P, 8, D], U8, name="xb", align_bytes=64)
        xs = const.tile([P, 8, 4], F32, name="xs")
        w1 = const.tile([P, 4096], U8, name="w1", align_bytes=64)
        w1s = const.tile([P, 2 * F], U8, name="w1s", align_bytes=64)
        w2 = const.tile([P, 2, 1024], U8, name="w2", align_bytes=64)
        w2s = const.tile([P, 2, D], U8, name="w2s", align_bytes=64)
        prm_a = const.tile([P, P], BF16, name="prm_a")
        prm_b = const.tile([P, P], BF16, name="prm_b")
        par = const.tile([P, 168], F32, name="par")
        wg = const.tile([P, 9, 8], F32, name="wg")
        warm = const.tile([P, 1], F32, name="warm")
        identf = const.tile([P, P], F32, name="identf", align_bytes=64)
        identb = const.tile([P, P], BF16, name="identb", align_bytes=64)
        perm = const.tile([P, P], F32, name="perm", align_bytes=64)
        xw = const.tile([P, 8, D], BF16, name="xw", align_bytes=64)
        xq = const.tile([P, T], U32, name="xq", align_bytes=64)
        xqs = const.tile([P, T], U8, name="xqs", align_bytes=64)
        us = []
        for k in range(4):
            us.append(const.tile([P, FLAT], F32, name="u%d" % k, align_bytes=64))
        unit_sets = []
        most = max(s + v for s, v in PLAN)
        for k in range(SETS):
            unit_sets.append([const.tile([P, T], F32, name="unit_%d_%d" % (k, j), align_bytes=64) for j in range(most)])
        g = const.tile([P, 8, 2, 2, 256], BF16, name="g", align_bytes=64)
        gq = const.tile([P, 2, T], U32, name="gq", align_bytes=64)
        gqs = const.tile([P, 2, T], U8, name="gqs", align_bytes=64)

        xv = x_bytes.rearrange("o a b k -> (o a b) k").rearrange("(p i) k -> p i k", i=8)
        xsv = x_scale.rearrange("o a b j -> (o a b) j").rearrange("(p i) j -> p i j", i=8)
        ov = out.rearrange("o a b n -> (o a b) n")
        wdv = wd.rearrange("r t (c p) -> (r t c) p", p=P)

        nc.scalar.dma_start(out=xs[:], in_=xsv)
        nc.vector.memset(w1s[:].bitcast(I32), 0)
        nc.vector.memset(warm[:], 0.0)
        nc.scalar.activation(out=warm[:], in_=warm[:], func=ACT.Silu)
        for m in range(2):
            nc.sync.dma_start(out=xb[:, 4 * m : 4 * m + 4, :], in_=xv[:, 4 * m : 4 * m + 4, :])
        nc.sync.dma_start(out=w1[:].bitcast(I32), in_=w1_words[0].bitcast(I32))
        for q in range(4):
            nc.sync.dma_start(out=w1s[32 * q : 32 * q + 4, :].bitcast(I32), in_=w1_scales[0, 4 * q : 4 * q + 4, :].bitcast(I32))
        nc.vector.memset(prm_b[:], 0.0)
        nc.sync.dma_start(out=prm_a[:], in_=wdv[0:P, :])
        nc.sync.dma_start(out=prm_b[0:16, :], in_=wdv[P : P + 16, :])
        nc.sync.dma_start(out=prm_b[16:32, :], in_=b1.rearrange("(c p) -> c p", p=P))
        nc.sync.dma_start(out=prm_b[32:40, :], in_=gain.rearrange("(c p) -> c p", p=P))
        nc.vector.memset(w2s[:].rearrange("p g n -> p (g n)").bitcast(I32), 0)
        nc.sync.dma_start(out=w2[:].rearrange("p g n -> p (g n)").bitcast(I32).rearrange("p (g n) -> p g n", g=2), in_=w2_words.bitcast(I32).rearrange("g p n -> p g n"))
        for q in range(4):
            nc.sync.dma_start(
                out=w2s[32 * q : 32 * q + 4, :, :].rearrange("p g n -> p (g n)").bitcast(I32).rearrange("p (g n) -> p g n", g=2),
                in_=w2_scales.bitcast(I32)[:, 4 * q : 4 * q + 4, :].rearrange("g q n -> q g n"),
            )

        make_identity(nc, identf[:])
        make_identity(nc, identb[:])
        for k in range(4):
            nc.vector.memset(us[k][:, 0 : ROW], 0.0)
            nc.vector.memset(us[k][:, ROW : 33 * ROW].rearrange("p (r w) -> p r w", w=ROW)[:, :, 0:LEFT], 0.0)
            nc.vector.memset(us[k][:, 33 * ROW : FLAT], 0.0)

        def widen(m):
            for i in (2 * m, 2 * m + 1):
                for j in range(4):
                    cols = slice(P * j, P * j + P)
                    if j < 3:
                        nc.vector.tensor_scalar(out=xw[:, i, cols], in0=xb[:, i, cols].bitcast(FP8), scalar1=xs[:, i, j : j + 1], scalar2=None, op0=MULT)
                    else:
                        nc.scalar.activation(out=xw[:, i, cols], in_=xb[:, i, cols].bitcast(FP8), func=ACT.Copy, scale=xs[:, i, j : j + 1])

        xt = {}
        xg = {}

        def x_turn(m):
            t = psum.tile([P, 2, 2, P], F32, name="xt_%d" % m, tag="b%d" % m, bufs=1)
            xt[m] = t
            for i2 in range(2):
                words = xw[:, 2 * m + i2, :].bitcast(F32)
                for u in range(2):
                    nc.tensor.transpose(t[:, i2, u, :], words[:, u:256:2], identf[:])

        def turn_copy(src, name, vector=False):
            dst = work.tile([P, 1024], BF16, name=name, tag="grouped", bufs=3, align_bytes=64)
            o = dst[:].bitcast(F32).rearrange("p (i r u) -> p i r u", i=2, u=2)
            s = src[:].rearrange("p i u r -> p i r u")
            if vector:
                nc.vector.tensor_copy(out=o, in_=s)
            else:
                nc.scalar.copy(out=o, in_=s)
            return dst

        def x_copy(m, vector=False):
            xg[m] = turn_copy(xt[m], "xg_%d" % m, vector)

        def x_quant(m):
            cols = slice(256 * m, 256 * m + 256)
            nc.vector.quantize_mx(out=xq[:, cols].bitcast(FP8X4), scales=xqs[:, cols], in_=xg[m][:])

        order = []
        for pr in range(8):
            order += [pr, 8 + pr]

        hs = {}

        def h_tile(n, half):
            hs[n, half] = psum.tile([P, 512], F32, name="h_%d_%d" % (n, half), tag="h%d" % half, bufs=1)

        def mx1(n, half, keep=0):
            c = order[n]
            h_tile(n, half)
            for j in range(keep):
                keep_clock(hs[n, half], j)
            h = hs[n, half]
            cols = slice(512 * half, 512 * half + 512)
            nc.tensor.matmul_mx(
                out=h[:],
                lhsT=w1[:, 256 * c : 256 * c + 256].bitcast(FP4X4),
                lhsT_scale=w1s[:, P * c : P * c + P],
                rhs=xq[:, cols].bitcast(FP8X4),
                rhs_scale=xqs[:, cols],
                start=True,
                stop=True,
            )

        def u_rows(n, base, count):
            return us[n % 4][:, base : base + ROW * count].rearrange("p (r w) -> p r w", w=ROW)[:, :, 0:32]

        def silu1(n, half):
            c = order[n]
            nc.scalar.activation(
                out=u_rows(n, ROW + LEFT, 32).rearrange("p a (b i) -> p a b i", i=8)[:, :, :, 4 * half : 4 * half + 4],
                in_=hs[n, half][:].rearrange("p (i a b) -> p a b i", i=4, b=4),
                func=ACT.Silu,
                bias=par[:, 144 + c : 145 + c],
            )

        units = {}
        for n in range(16):
            units[n] = unit_sets[n % SETS][: PLAN[n][0] + PLAN[n][1]]

        def tap_weight(n, tap):
            c = order[n]
            if c < 8:
                return wg[:, tap, c : c + 1]
            return par[:, 16 * tap + c : 16 * tap + c + 1]

        def tap_views(n, k, tap, lo, hi):
            r, t = divmod(tap, 3)
            dst = units[n][k][:, 32 * lo : 32 * hi].rearrange("p (r w) -> p r w", w=32)
            return u_rows(n, (r + lo) * ROW + LEFT - 1 + t, hi - lo), dst

        def s_product(n, k, lo=0, hi=32):
            if k < PLAN[n][0]:
                tap = TAPS[k]
                src, dst = tap_views(n, k, tap, lo, hi)
                nc.scalar.activation(out=dst, in_=src, func=ACT.Copy, scale=tap_weight(n, tap))

        def v_products(n, lo, hi, extra=()):
            s, v = PLAN[n]
            lists = split_taps(s, v)
            work_list = [(k, 0, lists[k][0]) for k in range(s, s + v)]
            for d in range(1, max(len(taps) for taps in lists)):
                for k, taps in enumerate(lists):
                    if d < len(taps):
                        work_list.append((k, d, taps[d]))
            for pos, (k, d, tap) in enumerate(work_list):
                src, dst = tap_views(n, k, tap, lo, hi)
                if d == 0:
                    nc.vector.tensor_scalar(out=dst, in0=src, scalar1=tap_weight(n, tap), scalar2=None, op0=MULT)
                else:
                    nc.vector.scalar_tensor_tensor(out=dst, in0=src, scalar=tap_weight(n, tap), in1=dst, op0=MULT, op1=ADD)
                for at, fn in extra:
                    if min(at, len(work_list) - 1) == pos:
                        fn()

        accs = {}

        def acc_tile(n, part, parts):
            bank = (2 * n + part) % 5 if parts == 2 else part
            accs[n, part] = psum.tile([P, T // parts], F32, name="acc_%d_%d" % (n, part), tag="b%d" % bank, bufs=1)

        def gather_tile(n, part, j, parts=2):
            if j == 0:
                acc_tile(n, part, parts)
            acc = accs[n, part]
            lo = T // parts * part + P * j
            count = len(units[n])
            for k in range(count):
                nc.tensor.matmul(
                    acc[:, P * j : P * j + P], lhsT=units[n][k][:, lo : lo + P], rhs=perm[:],
                    start=(k == 0), stop=(k == count - 1), is_transpose=True,
                )

        def gather(n, part, parts=2):
            for j in range(8 // parts):
                gather_tile(n, part, j, parts)

        def keep_clock(bank, j):
            nc.tensor.matmul(bank[:, P * j : P * j + P], lhsT=identf[:], rhs=identf[:], start=True, stop=True)

        sgs = {}

        def gate_silu(pr, part, parts=2):
            width = T // parts
            sg = work.tile([P, width], F32, name="sg_%d_%d" % (pr, part), tag="sg", bufs=4, align_bytes=64)
            sgs[pr, part] = sg
            nc.scalar.activation(out=sg[:], in_=accs[2 * pr + 1, part][:], func=ACT.Silu)

        def gate_mul(pr, part, parts=2):
            q, c4 = divmod(pr, 4)
            tiles = 8 // parts
            half, start = divmod(tiles * part, 4)
            nc.vector.tensor_tensor(
                out=g[:, tiles * part : tiles * part + tiles, q, :, 64 * c4 : 64 * c4 + 64],
                in0=accs[2 * pr, half][:, P * start : P * start + P * tiles].rearrange("p (i u w) -> p i u w", i=tiles, u=2),
                in1=sgs[pr, part][:].rearrange("p (i u w) -> p i u w", i=tiles, u=2),
                op=MULT,
            )

        gt = {}
        gg = {}

        def g_turn(q, m):
            t = psum.tile([P, 2, 2, P], F32, name="gt_%d_%d" % (q, m), tag="tp" if q == 0 else ("h0", "h1", "tp", "h0")[m], bufs=1)
            gt[q, m] = t
            for i2 in range(2):
                for u in range(2):
                    nc.tensor.transpose(t[:, i2, u, :], g[:, 2 * m + i2, q, u, :].bitcast(F32), identf[:])

        def g_copy(q, m, vector=True):
            gg[q, m] = turn_copy(gt[q, m], "gg_%d_%d" % (q, m), vector)

        def g_quant(q, m):
            cols = slice(256 * m, 256 * m + 256)
            nc.vector.quantize_mx(out=gq[:, q, cols].bitcast(FP8X4), scales=gqs[:, q, cols], in_=gg[q, m][:])

        outs = {}
        out_tags = ("b0", "b1", "h1", "b2", "b3", "b4", "b0", "b1")

        def mx2(i, q):
            if q == 0:
                outs[i] = psum.tile([P, D], F32, name="o_%d" % i, tag=out_tags[i], bufs=1)
            tok = slice(P * i, P * i + P)
            nc.tensor.matmul_mx(
                out=outs[i][:],
                lhsT=gq[:, q, tok].bitcast(FP8X4),
                lhsT_scale=gqs[:, q, tok],
                rhs=w2[:, q, :].bitcast(FP4X4),
                rhs_scale=w2s[:, q, :],
                start=(q == 0),
                stop=(q == 1),
            )

        def store(i):
            ob = work.tile([P, D], F32, name="ob_%d" % i, tag="ob", bufs=8, align_bytes=64)
            if i % 2 == 0:
                nc.scalar.copy(out=ob[:], in_=outs[i][:])
            else:
                nc.vector.tensor_copy(out=ob[:], in_=outs[i][:])
            nc.sync.dma_start(out=ov[P * i : P * i + P, :], in_=ob[:])

        spare = psum.tile([P, 512], F32, name="spare", tag="b4", bufs=1)
        for k in range(HEAD_KEEP):
            keep_clock(spare, k % 4)
        nc.vector.tensor_copy(out=perm[:].rearrange("q (u p e) -> q u p e", u=2, e=2), in_=identf[:].rearrange("q (p u e) -> q u p e", u=2, e=2))
        for m in range(4):
            widen(m)
            x_turn(m)
        pt = psum.tile([P, 2, P], BF16, name="pt", tag="tp", bufs=1)
        nc.tensor.transpose(pt[:, 0, :], prm_a[:], identb[:])
        nc.tensor.transpose(pt[:, 1, :], prm_b[:], identb[:])
        for m in range(3):
            x_copy(m)
            x_quant(m)
            if m == 1:
                nc.vector.tensor_copy(out=par[:], in_=pt[:].rearrange("p a b -> p (a b)")[:, 0:168])
        mx1(0, 0)
        x_copy(3)
        x_quant(3)
        nc.vector.tensor_tensor(
            out=wg[:],
            in0=par[:, 0:144].rearrange("p (k c) -> p k c", c=16)[:, :, 0:8],
            in1=par[:, 160:168].unsqueeze(1).to_broadcast([P, 9, 8]),
            op=MULT,
        )
        silu1(0, 0)
        mx1(0, 1)
        silu1(0, 1)
        mx1(1, 0)
        mx1(1, 1)

        for n in range(16):
            pr = n // 2 - 1
            gate = n % 2 == 1 and pr >= 0
            extra = []
            if n >= 1:
                gather_tile(n - 1, 0, 0)
                gather_tile(n - 1, 0, 1)
                for j in range(KEEP_A):
                    keep_clock(accs[n - 1, 0], 2 + j)
                gather_tile(n - 1, 0, 2)
                gather_tile(n - 1, 0, 3)
            if n < 15:
                silu1(n + 1, 0)
            if gate:
                gate_silu(pr, 0)
                extra = [(1, lambda: gate_mul(pr, 0)), (3, lambda: gate_mul(pr, 1))]
            if n < 15:
                s_product(n, 0)
                silu1(n + 1, 1)
                if gate:
                    gate_silu(pr, 1)
                for k in range(1, 6):
                    s_product(n, k)
            else:
                for k in range(3):
                    s_product(n, k, 0, 16)
                gate_silu(pr, 1)
                for k in range(3, 6):
                    s_product(n, k, 0, 16)
                for k in range(6):
                    s_product(n, k, 16, 32)
            v_products(n, 0, 32 if n < 15 else 16, extra)
            if 10 <= n <= 13:
                g_copy(0, n - 10, VCOPY)
            if n >= 1:
                gather_tile(n - 1, 1, 0)
            if n < 14:
                mx1(n + 2, 0, KEEP_0)
            else:
                for j in range(LATE_KEEP):
                    keep_clock(accs[n - 1, 1], 1 + j)
            if n >= 1:
                for j in range(1, 4):
                    gather_tile(n - 1, 1, j)
            if n < 14:
                mx1(n + 2, 1, KEEP_1)
            if 11 <= n <= 14:
                g_quant(0, n - 11)
            if 9 <= n <= 12:
                g_turn(0, n - 9)
        for m in range(2):
            gather(15, m, 4)
            gate_silu(7, m, 4)
        v_products(15, 16, 32, [(G0, lambda: gate_mul(7, 0, 4)), (G1, lambda: gate_mul(7, 1, 4))])

        g_turn(1, 0)
        g_copy(1, 0, False)
        g_turn(1, 1)
        g_copy(1, 1, False)
        gather(15, 2, 4)
        gate_silu(7, 2, 4)
        gather(15, 3, 4)
        gate_silu(7, 3, 4)
        g_quant(1, 0)
        gate_mul(7, 2, 4)
        g_quant(1, 1)
        gate_mul(7, 3, 4)
        for i in range(2):
            mx2(i, 0)
            mx2(i, 1)
        store(0)
        g_turn(1, 2)
        g_turn(1, 3)
        g_copy(1, 2, False)
        g_copy(1, 3, True)
        store(1)
        for i in (2, 3):
            mx2(i, 0)
            mx2(i, 1)
        g_quant(1, 2)
        store(2)
        g_quant(1, 3)
        store(3)
        for i in range(4, 8):
            mx2(i, 0)
        for i in range(4, 8):
            mx2(i, 1)
            store(i)
